import numpy as np, ml_dtypes
CORES = [61,69,101,62,70,102]
N = 6
W, KW, DIL = 256, 3, 2
H = (KW // 2) * DIL
def setup_inputs(rng):
    return {"x": rng.standard_normal((N, 128, W), dtype=np.float32).astype(ml_dtypes.bfloat16), "w": rng.standard_normal((N, 128, KW * 128), dtype=np.float32).astype(ml_dtypes.bfloat16)}
def setup_inputs_big(rng):
    d = setup_inputs(rng)
    for k in ("x", "w"): d[k] = (d[k].astype(np.float32) * 1024.0).astype(d[k].dtype)
    return d
def setup_inputs_small(rng):
    d = setup_inputs(rng)
    for k in ("x", "w"): d[k] = (d[k].astype(np.float32) * (1 / 1024.0)).astype(d[k].dtype)
    return d
def reference(x, w):
    X, W_ = x.astype(np.float64), w.astype(np.float64)
    g = np.concatenate(list(X), axis=1)
    p = np.pad(g, ((0, 0), (H, H)))
    y = np.zeros((N, 128, W))
    for r in range(N):
        for i in range(KW):
            y[r] += W_[r][:, 128 * i:128 * i + 128].T @ p[:, W * r + i * DIL:W * r + i * DIL + W]
    return {"y": y.astype(ml_dtypes.bfloat16 if x.dtype != np.float64 else np.float64)}

@@ -1,0 +1,191 @@
+from concourse.bass import DstId, RemoteDMATransfer
+
+LAND_DRAM = True
+K_LAND = 8
+
+BF = "bfloat16"
+SCRATCH = {
+    "xs": ("sbuf", [128, 256], BF),
+    "ws": ("sbuf", [128, 384], BF),
+    "yi": ("sbuf", [128, 256], BF),
+    "hl": ("sbuf", [128, 8], BF),
+    "hr": ("sbuf", [128, 8], BF),
+    "yl": ("sbuf", [128, 8], BF),
+    "yr": ("sbuf", [128, 8], BF),
+    "el": ("dram", [128, 2], BF),
+    "er": ("dram", [128, 2], BF),
+    "rl": ("dram", [128, 2], BF),
+    "dl": ("dram", [128, 2], BF),
+    "dr": ("dram", [128, 2], BF),
+    "pi": ("psum", [128, 512], "float32"),
+    "pl": ("psum", [128, 512], "float32"),
+    "pr": ("psum", [128, 512], "float32"),
+}
+SEMAPHORES = ["sel", "ser", "sx", "sw", "ra", "al", "ar", "sent", "hll", "hlr",
+              "mi", "ml", "mr", "ci", "cl", "cr", "oi", "ol", "orr"]
+
+
+def _bits(mask, k, skip=0):
+    out, b = 0, 0
+    while k > 0:
+        if (mask >> b) & 1:
+            if skip > 0:
+                skip -= 1
+            else:
+                out |= 1 << b
+                k -= 1
+        b += 1
+    return out
+
+
+def _plan(T, topo):
+    cores = list(T.cores)
+    n = len(cores)
+    msgs = []
+    for r in range(n):
+        for edge, q in (("r", r + 1), ("l", r - 1)):
+            if not 0 <= q < n:
+                continue
+            s, d = cores[r], cores[q]
+            via = None
+            if not topo.may_write(s, d):
+                c = [c for c in cores if c != s and c != d and topo.chip(c) == topo.chip(s) and topo.may_write(c, d)]
+                c.sort(key=lambda k: topo.die(k) != topo.die(s))
+                via = c[0]
+            msgs.append({"src": s, "dst": d, "edge": edge, "halo": "l" if edge == "r" else "r", "via": via})
+    for m in msgs:
+        if LAND_DRAM:
+            m["k"] = 1
+        elif m["via"] is not None:
+            m["k"] = K_LAND
+        else:
+            m["k"] = K_LAND // len([o for o in msgs if o["src"] == m["src"] and o["via"] is None])
+    return msgs
+
+
+def rank_program(g, core, T, topo):
+    rank = T.rank_of(core)
+    if rank is None:
+        return
+    S = T.sem
+    msgs = _plan(T, topo)
+    own = [m for m in msgs if m["src"] == core]
+    own.sort(key=lambda m: m["via"] is None)
+    jobs = [m for m in msgs if m["via"] == core]
+    assert len(jobs) <= 1
+    inc = {m["halo"]: m for m in msgs if m["dst"] == core}
+    sides = sorted(inc, key=lambda h: inc[h]["via"] is not None)
+    late, early = sides[-1], sides[:-1]
+    W = 256
+    xcol = {"l": (0, 2), "r": (W - 2, W)}
+    esem = {"l": S.sel, "r": S.ser}
+    ebuf = {"l": T.el, "r": T.er}
+    asem = {"l": S.al, "r": S.ar}
+    dbuf = {"l": T.dl, "r": T.dr}
+    hbuf = {"l": T.hl, "r": T.hr}
+    hsem = {"l": S.hll, "r": S.hlr}
+    msem = {"l": S.ml, "r": S.mr}
+    csem = {"l": S.cl, "r": S.cr}
+    osem = {"l": S.ol, "r": S.orr}
+    pbuf = {"l": T.pl, "r": T.pr}
+    ybuf = {"l": T.yl, "r": T.yr}
+    sy, sc, te, ve = g.sync, g.scalar, g.tensor, g.vector
+
+    def load_edge(q, m):
+        a, b = xcol[m["edge"]]
+        q.dma_start(ebuf[m["edge"]][:, :], T.x[:, a:b]).then_inc(esem[m["edge"]], 16)
+
+    load_edge(sy, own[0])
+    if len(own) == 2:
+        load_edge(sc, own[1])
+        sy.dma_start(T.xs[:, :], T.x[:, :]).then_inc(S.sx, 16)
+        sc.dma_start(T.ws[:, :], T.w[:, :]).then_inc(S.sw, 16)
+    else:
+        sy.dma_start(T.xs[:, :], T.x[:, :]).then_inc(S.sx, 16)
+        sy.dma_start(T.ws[:, :], T.w[:, :]).then_inc(S.sw, 16)
+
+    def landing(m):
+        return dbuf[m["halo"]][:, :] if LAND_DRAM else hbuf[m["halo"]][:, 0:2]
+
+    sent = 0
+    for m in own:
+        if m["via"] is None:
+            continue
+        g.wait_ge(esem[m["edge"]], 16)
+        rid, pid, _ = topo.addr(m["via"])
+        g.remote_dma(out_ap=T.rl[:, :], in_ap=ebuf[m["edge"]][:, :], remote_sem=S.ra, local_sem=S.sent,
+                     pid=pid, routing_id=rid, dma_engine_mask=_bits(topo.mask(core, m["via"]), 1))
+        sent += 1
+    direct = [m for m in own if m["via"] is None]
+    for m in direct:
+        g.wait_ge(esem[m["edge"]], 16)
+    if len(direct) == 1:
+        m = direct[0]
+        rid, pid, _ = topo.addr(m["dst"])
+        g.remote_dma(out_ap=landing(m), in_ap=ebuf[m["edge"]][:, :], remote_sem=asem[m["halo"]], local_sem=S.sent,
+                     pid=pid, routing_id=rid, dma_engine_mask=_bits(topo.mask(core, m["dst"]), m["k"]))
+        sent += m["k"]
+    elif direct:
+        trs, skip = [], 0
+        for m in direct:
+            rid, pid, _ = topo.addr(m["dst"])
+            trs.append(RemoteDMATransfer(dst_ids=[DstId(rid=rid, pnc=pid)],
+                                         dma_engine_mask=_bits(topo.mask(core, m["dst"]), m["k"], skip),
+                                         remote_sem=asem[m["halo"]], src=ebuf[m["edge"]][:, :], dst=landing(m)))
+            skip += m["k"]
+            sent += m["k"]
+        g.remote_dma_fused(trs, local_sem=S.sent)
+    for m in jobs:
+        g.wait_ge(S.ra, 1)
+        rid, pid, _ = topo.addr(m["dst"])
+        g.remote_dma(out_ap=landing(m), in_ap=T.rl[:, :], remote_sem=asem[m["halo"]], local_sem=S.sent,
+                     pid=pid, routing_id=rid, dma_engine_mask=_bits(topo.mask(core, m["dst"]), m["k"]))
+        sent += m["k"]
+    g.wait_ge(S.sent, sent)
+
+    w0, w1, w2 = T.ws[:, 0:128], T.ws[:, 128:256], T.ws[:, 256:384]
+    lo = 2 if "l" in inc else 0
+    hi = W - 2 if "r" in inc else W
+    a0, b2 = max(lo, 2), min(hi, W - 2)
+    te.wait_ge(S.sx, 16)
+    te.wait_ge(S.sw, 16)
+    te.matmul(T.pi[:, lo:hi], w1, T.xs[:, lo:hi], True, False)
+    te.matmul(T.pi[:, a0:hi], w0, T.xs[:, a0 - 2:hi - 2], False, False)
+    te.matmul(T.pi[:, lo:b2], w2, T.xs[:, lo + 2:b2 + 2], False, True).then_inc(S.mi, 1)
+    if "l" in inc:
+        te.matmul(T.pl[:, 0:2], w1, T.xs[:, 0:2], True, False)
+        te.matmul(T.pl[:, 0:2], w2, T.xs[:, 2:4], False, False)
+    if "r" in inc:
+        te.matmul(T.pr[:, 0:2], w1, T.xs[:, W - 2:W], True, False)
+        te.matmul(T.pr[:, 0:2], w0, T.xs[:, W - 4:W - 2], False, False)
+    for h in sides:
+        if LAND_DRAM:
+            te.wait_ge(hsem[h], 16)
+        else:
+            te.wait_ge(asem[h], inc[h]["k"])
+        te.matmul(pbuf[h][:, 0:2], w0 if h == "l" else w2, hbuf[h][:, 0:2], False, True).then_inc(msem[h], 1)
+
+    ve.wait_ge(S.mi, 1)
+    ve.tensor_copy(T.yi[:, lo:hi], T.pi[:, lo:hi]).then_inc(S.ci, 1)
+    for h in sides:
+        ve.wait_ge(msem[h], 1)
+        ve.tensor_copy(ybuf[h][:, 0:2], pbuf[h][:, 0:2]).then_inc(csem[h], 1)
+
+    def finish(q, h):
+        if LAND_DRAM:
+            q.wait_ge(asem[h], inc[h]["k"])
+            q.dma_start(hbuf[h][:, 0:2], dbuf[h][:, :]).then_inc(hsem[h], 16)
+        q.wait_ge(csem[h], 1)
+        a, b = xcol[h]
+        q.dma_start(T.y[:, a:b], ybuf[h][:, 0:2]).then_inc(osem[h], 16)
+
+    qi = sy if early else sc
+    qi.wait_ge(S.ci, 1)
+    qi.dma_start(T.y[:, lo:hi], T.yi[:, lo:hi]).then_inc(S.oi, 16)
+    for h in early:
+        finish(sc, h)
+    finish(sy, late)
+    for h in early:
+        sc.wait_ge(osem[h], 16)
+    qi.wait_ge(S.oi, 16)
+    sy.wait_ge(osem[late], 16)

@@ -1,6 +1,6 @@
 from concourse.bass import DstId, RemoteDMATransfer
 
-LAND_DRAM = True
+LAND_DRAM = False
 K_LAND = 8
 
 BF = "bfloat16"

from concourse.bass import DstId, RemoteDMATransfer

LAND_DRAM = False
K_LAND = 8

BF = "bfloat16"
SCRATCH = {
    "xs": ("sbuf", [128, 256], BF),
    "ws": ("sbuf", [128, 384], BF),
    "yi": ("sbuf", [128, 256], BF),
    "hl": ("sbuf", [128, 8], BF),
    "hr": ("sbuf", [128, 8], BF),
    "yl": ("sbuf", [128, 8], BF),
    "yr": ("sbuf", [128, 8], BF),
    "el": ("dram", [128, 2], BF),
    "er": ("dram", [128, 2], BF),
    "rl": ("dram", [128, 2], BF),
    "dl": ("dram", [128, 2], BF),
    "dr": ("dram", [128, 2], BF),
    "pi": ("psum", [128, 512], "float32"),
    "pl": ("psum", [128, 512], "float32"),
    "pr": ("psum", [128, 512], "float32"),
}
SEMAPHORES = ["sel", "ser", "sx", "sw", "ra", "al", "ar", "sent", "hll", "hlr",
              "mi", "ml", "mr", "ci", "cl", "cr", "oi", "ol", "orr"]


def _bits(mask, k, skip=0):
    out, b = 0, 0
    while k > 0:
        if (mask >> b) & 1:
            if skip > 0:
                skip -= 1
            else:
                out |= 1 << b
                k -= 1
        b += 1
    return out


def _plan(T, topo):
    cores = list(T.cores)
    n = len(cores)
    msgs = []
    for r in range(n):
        for edge, q in (("r", r + 1), ("l", r - 1)):
            if not 0 <= q < n:
                continue
            s, d = cores[r], cores[q]
            via = None
            if not topo.may_write(s, d):
                c = [c for c in cores if c != s and c != d and topo.chip(c) == topo.chip(s) and topo.may_write(c, d)]
                c.sort(key=lambda k: topo.die(k) != topo.die(s))
                via = c[0]
            msgs.append({"src": s, "dst": d, "edge": edge, "halo": "l" if edge == "r" else "r", "via": via})
    for m in msgs:
        if LAND_DRAM:
            m["k"] = 1
        elif m["via"] is not None:
            m["k"] = K_LAND
        else:
            m["k"] = K_LAND // len([o for o in msgs if o["src"] == m["src"] and o["via"] is None])
    return msgs


def rank_program(g, core, T, topo):
    rank = T.rank_of(core)
    if rank is None:
        return
    S = T.sem
    msgs = _plan(T, topo)
    own = [m for m in msgs if m["src"] == core]
    own.sort(key=lambda m: m["via"] is None)
    jobs = [m for m in msgs if m["via"] == core]
    assert len(jobs) <= 1
    inc = {m["halo"]: m for m in msgs if m["dst"] == core}
    sides = sorted(inc, key=lambda h: inc[h]["via"] is not None)
    late, early = sides[-1], sides[:-1]
    W = 256
    xcol = {"l": (0, 2), "r": (W - 2, W)}
    esem = {"l": S.sel, "r": S.ser}
    ebuf = {"l": T.el, "r": T.er}
    asem = {"l": S.al, "r": S.ar}
    dbuf = {"l": T.dl, "r": T.dr}
    hbuf = {"l": T.hl, "r": T.hr}
    hsem = {"l": S.hll, "r": S.hlr}
    msem = {"l": S.ml, "r": S.mr}
    csem = {"l": S.cl, "r": S.cr}
    osem = {"l": S.ol, "r": S.orr}
    pbuf = {"l": T.pl, "r": T.pr}
    ybuf = {"l": T.yl, "r": T.yr}
    sy, sc, te, ve = g.sync, g.scalar, g.tensor, g.vector

    def load_edge(q, m):
        a, b = xcol[m["edge"]]
        q.dma_start(ebuf[m["edge"]][:, :], T.x[:, a:b]).then_inc(esem[m["edge"]], 16)

    load_edge(sy, own[0])
    if len(own) == 2:
        load_edge(sc, own[1])
        sy.dma_start(T.xs[:, :], T.x[:, :]).then_inc(S.sx, 16)
        sc.dma_start(T.ws[:, :], T.w[:, :]).then_inc(S.sw, 16)
    else:
        sy.dma_start(T.xs[:, :], T.x[:, :]).then_inc(S.sx, 16)
        sy.dma_start(T.ws[:, :], T.w[:, :]).then_inc(S.sw, 16)

    def landing(m):
        return dbuf[m["halo"]][:, :] if LAND_DRAM else hbuf[m["halo"]][:, 0:2]

    sent = 0
    for m in own:
        if m["via"] is None:
            continue
        g.wait_ge(esem[m["edge"]], 16)
        rid, pid, _ = topo.addr(m["via"])
        g.remote_dma(out_ap=T.rl[:, :], in_ap=ebuf[m["edge"]][:, :], remote_sem=S.ra, local_sem=S.sent,
                     pid=pid, routing_id=rid, dma_engine_mask=_bits(topo.mask(core, m["via"]), 1))
        sent += 1
    direct = [m for m in own if m["via"] is None]
    for m in direct:
        g.wait_ge(esem[m["edge"]], 16)
    if len(direct) == 1:
        m = direct[0]
        rid, pid, _ = topo.addr(m["dst"])
        g.remote_dma(out_ap=landing(m), in_ap=ebuf[m["edge"]][:, :], remote_sem=asem[m["halo"]], local_sem=S.sent,
                     pid=pid, routing_id=rid, dma_engine_mask=_bits(topo.mask(core, m["dst"]), m["k"]))
        sent += m["k"]
    elif direct:
        trs, skip = [], 0
        for m in direct:
            rid, pid, _ = topo.addr(m["dst"])
            trs.append(RemoteDMATransfer(dst_ids=[DstId(rid=rid, pnc=pid)],
                                         dma_engine_mask=_bits(topo.mask(core, m["dst"]), m["k"], skip),
                                         remote_sem=asem[m["halo"]], src=ebuf[m["edge"]][:, :], dst=landing(m)))
            skip += m["k"]
            sent += m["k"]
        g.remote_dma_fused(trs, local_sem=S.sent)
    for m in jobs:
        g.wait_ge(S.ra, 1)
        rid, pid, _ = topo.addr(m["dst"])
        g.remote_dma(out_ap=landing(m), in_ap=T.rl[:, :], remote_sem=asem[m["halo"]], local_sem=S.sent,
                     pid=pid, routing_id=rid, dma_engine_mask=_bits(topo.mask(core, m["dst"]), m["k"]))
        sent += m["k"]
    g.wait_ge(S.sent, sent)

    w0, w1, w2 = T.ws[:, 0:128], T.ws[:, 128:256], T.ws[:, 256:384]
    lo = 2 if "l" in inc else 0
    hi = W - 2 if "r" in inc else W
    a0, b2 = max(lo, 2), min(hi, W - 2)
    te.wait_ge(S.sx, 16)
    te.wait_ge(S.sw, 16)
    te.matmul(T.pi[:, lo:hi], w1, T.xs[:, lo:hi], True, False)
    te.matmul(T.pi[:, a0:hi], w0, T.xs[:, a0 - 2:hi - 2], False, False)
    te.matmul(T.pi[:, lo:b2], w2, T.xs[:, lo + 2:b2 + 2], False, True).then_inc(S.mi, 1)
    if "l" in inc:
        te.matmul(T.pl[:, 0:2], w1, T.xs[:, 0:2], True, False)
        te.matmul(T.pl[:, 0:2], w2, T.xs[:, 2:4], False, False)
    if "r" in inc:
        te.matmul(T.pr[:, 0:2], w1, T.xs[:, W - 2:W], True, False)
        te.matmul(T.pr[:, 0:2], w0, T.xs[:, W - 4:W - 2], False, False)
    for h in sides:
        if LAND_DRAM:
            te.wait_ge(hsem[h], 16)
        else:
            te.wait_ge(asem[h], inc[h]["k"])
        te.matmul(pbuf[h][:, 0:2], w0 if h == "l" else w2, hbuf[h][:, 0:2], False, True).then_inc(msem[h], 1)

    ve.wait_ge(S.mi, 1)
    ve.tensor_copy(T.yi[:, lo:hi], T.pi[:, lo:hi]).then_inc(S.ci, 1)
    for h in sides:
        ve.wait_ge(msem[h], 1)
        ve.tensor_copy(ybuf[h][:, 0:2], pbuf[h][:, 0:2]).then_inc(csem[h], 1)

    def finish(q, h):
        if LAND_DRAM:
            q.wait_ge(asem[h], inc[h]["k"])
            q.dma_start(hbuf[h][:, 0:2], dbuf[h][:, :]).then_inc(hsem[h], 16)
        q.wait_ge(csem[h], 1)
        a, b = xcol[h]
        q.dma_start(T.y[:, a:b], ybuf[h][:, 0:2]).then_inc(osem[h], 16)

    qi = sy if early else sc
    qi.wait_ge(S.ci, 1)
    qi.dma_start(T.y[:, lo:hi], T.yi[:, lo:hi]).then_inc(S.oi, 16)
    for h in early:
        finish(sc, h)
    finish(sy, late)
    for h in early:
        sc.wait_ge(osem[h], 16)
    qi.wait_ge(S.oi, 16)
    sy.wait_ge(osem[late], 16)
